import numpy as np
import ml_dtypes


def mxq(x, axis, fmt="e4m3"):
    dtype, down = {"e4m3": (ml_dtypes.float8_e4m3fn, 7), "e5m2": (ml_dtypes.float8_e5m2, 14)}[fmt]
    v = np.moveaxis(np.asarray(x, np.float32).astype(ml_dtypes.bfloat16).astype(np.float64), axis, -1)
    blocks = v.reshape(v.shape[:-1] + (-1, 32))
    amax = np.abs(blocks).max(-1, keepdims=True)
    byte = np.maximum(np.where(amax > 0, np.frexp(amax)[1] - 1 + 127, 0) - down, 1)
    scale = np.exp2(byte - 127.0)
    codes = (blocks / scale).astype(np.float32).astype(dtype).astype(np.float64)
    return np.moveaxis((codes * scale).reshape(v.shape), -1, axis)


WIDE = False


def mx_kscale(k):
    if not WIDE:
        return np.ones(k)
    levels = np.array([10, -10, 5, -5, 0])
    if k % 512:
        return np.exp2(np.random.permutation(np.resize(levels, k // 32))).repeat(32)
    a = np.empty((k // 512, 16))
    for p in range(k // 512):
        a[p, :8] = np.random.permutation(np.resize(levels, 8))
        for g in range(8):
            far = levels[np.abs(levels - a[p, g]) >= 10]
            a[p, g + 8] = far[np.random.randint(len(far))]
    return np.exp2(a.ravel()).repeat(32)


def f64(x):
    return np.asarray(x).astype(np.float64)


def striped8(idx):
    return np.asarray(idx).reshape(8, -1, 16).transpose(0, 2, 1).reshape(128, -1).astype(np.uint16)


def unstriped8(offs):
    return offs.reshape(8, 16, -1).transpose(0, 2, 1).reshape(8, -1).astype(np.int64)


def pick8(x, idx, run):
    r = np.arange(len(x))
    return x[r[:, None], idx[r % (8 * run) // run]]


D, T, I, Q, X, E = 512, 2048, 512, 256, 32, 512


def setup_inputs():
    n = np.random.standard_normal
    idx = np.stack([np.random.permutation(T)[:I] for _ in range(8)])
    fd = mx_kscale(D)
    fi = mx_kscale(I)
    ti = np.ones((8, T))
    np.put_along_axis(ti, idx, np.tile(fi, (8, 1)), axis=1)
    return {
        "query": (n((D, Q)) * (np.arange(D)[:, None] // 64 == np.arange(Q) % 8) * 0.0625 * fd[:, None]).astype(np.float32),
        "keys": (n((D, T)) / fd[:, None]).astype(np.float32),
        "size": (np.random.uniform(0.5, 2.0, (1, I)) * fi).astype(np.float32),
        "vals": (n((E, T)) / ti[np.arange(E) % 512 // 64]).astype(np.float32),
        "own": ((np.arange(E)[:, None] // 64 == np.arange(Q) % 8) * 1.0).astype(np.float32),
        "offs": striped8(idx),
    }


def reference(query, keys, size, vals, own, offs):
    idx = unstriped8(offs)
    queryq = mxq(f64(query), 0, "e4m3")
    keysidxq = mxq(pick8(f64(keys), idx, 64), 0, "e4m3")
    a = queryq.T @ keysidxq
    p = np.exp(a - np.max(a, axis=1, keepdims=True))
    w = p * f64(size) / np.sum(p, axis=1, keepdims=True)
    wt = w.T
    vt = pick8(f64(vals), idx, 64).T
    vtq = mxq(vt, 0, "e4m3")
    wtq = mxq(wt, 0, "e4m3")
    o = vtq.T @ wtq
    ob = o * f64(own)
    y = ob.reshape(E, X, Q // X).sum(axis=2)
    return y

@@ -1,0 +1,130 @@
+from contextlib import ExitStack
+
+import concourse.mybir as mybir
+from concourse.masks import make_identity
+
+D, T, I, Q, X, E = 512, 2048, 512, 256, 32, 512
+FLOPS = 2 * Q * I * D + 2 * E * Q * I
+
+F32 = mybir.dt.float32
+BF16 = mybir.dt.bfloat16
+U32 = mybir.dt.uint32
+U16 = mybir.dt.uint16
+U8 = mybir.dt.uint8
+FP8X4 = mybir.dt.float8_e4m3fn_x4
+ALU = mybir.AluOpType
+ACT = mybir.ActivationFunctionType
+AXIS = mybir.AxisListType
+
+P = 128
+PACK = 4
+HEADS = Q // X
+QT = Q // P
+
+
+def tile_attend_ownlists_heads_kernel(tc, query, keys, size, vals, own, offs, out):
+    nc = tc.nc
+    with ExitStack() as ctx:
+        sb = ctx.enter_context(tc.tile_pool(name="sb", bufs=1))
+        ps = ctx.enter_context(tc.psum_pool(name="ps", bufs=1))
+
+        lists = sb.tile([P, I // 16], U16, name="lists")
+        nc.sync.dma_start(lists[:], offs)
+        size_col = sb.tile([P, PACK], F32, name="size_col")
+        nc.sync.dma_start(size_col[:], size.rearrange("o (p j) -> (o p) j", j=PACK))
+
+        keys_v = keys.rearrange("(p j) t -> p j t", j=PACK)
+        vals_v = vals.rearrange("(p j) t -> p j t", j=PACK)
+        key_pool = []
+        for j in range(PACK):
+            kp = sb.tile([P, T], F32, name="key_pool%d" % j)
+            nc.sync.dma_start(kp[:], keys_v[:, j, :])
+            key_pool.append(kp)
+        q_raw = sb.tile([P, PACK, Q], F32, name="q_raw")
+        nc.sync.dma_start(q_raw[:], query.rearrange("(p j) q -> p j q", j=PACK))
+        val_pool = []
+        for j in range(PACK):
+            vp = sb.tile([P, T], F32, name="val_pool%d" % j)
+            nc.sync.dma_start(vp[:], vals_v[:, j, :])
+            val_pool.append(vp)
+        own_sb = sb.tile([P, PACK, Q], F32, name="own_sb")
+        nc.sync.dma_start(own_sb[:], own.rearrange("(p j) q -> p j q", j=PACK))
+
+        ident = sb.tile([P, P], F32, name="ident")
+        make_identity(nc, ident[:])
+
+        warm_in = sb.tile([P, 1], F32, name="warm_in")
+        warm_out = sb.tile([P, 1], F32, name="warm_out")
+        nc.vector.memset(warm_in[:], 0.0)
+        nc.scalar.activation(warm_out[:], warm_in[:], ACT.Exp)
+
+        size_ps = ps.tile([P, PACK, P], F32, name="size_ps", tag="bank_a")
+        for j in range(PACK):
+            nc.tensor.transpose(size_ps[:, j, :], size_col[:, j : j + 1].to_broadcast([P, P]), ident[:])
+        size_all = sb.tile([P, P, PACK], F32, name="size_all")
+        nc.scalar.copy(size_all[:], size_ps[:].rearrange("p j s -> p s j"))
+
+        k_grouped = sb.tile([P, I, PACK], BF16, name="k_grouped", align_bytes=64)
+        for j in range(PACK):
+            k_picked = sb.tile([P, I], BF16, name="k_picked%d" % j)
+            nc.vector.tensor_copy(k_picked[:], key_pool[j][:].indirect(lists[:]))
+            nc.vector.tensor_copy(k_grouped[:, :, j], k_picked[:])
+        k_codes = sb.tile([P, I], U32, name="k_codes", align_bytes=64)
+        k_scales = sb.tile([P, I], U8, name="k_scales", align_bytes=64)
+        nc.vector.quantize_mx(out=k_codes[:].bitcast(FP8X4), scales=k_scales[:], in_=k_grouped[:].rearrange("p i j -> p (i j)"))
+
+        scores = []
+        for m in range(QT):
+            q_grouped = sb.tile([P, P, PACK], BF16, name="q_grouped%d" % m, align_bytes=64)
+            nc.scalar.copy(q_grouped[:], q_raw[:, :, m * P : (m + 1) * P].rearrange("p j q -> p q j"))
+            q_codes = sb.tile([P, P], U32, name="q_codes%d" % m, align_bytes=64)
+            q_scales = sb.tile([P, P], U8, name="q_scales%d" % m, align_bytes=64)
+            nc.vector.quantize_mx(out=q_codes[:].bitcast(FP8X4), scales=q_scales[:], in_=q_grouped[:].rearrange("p q j -> p (q j)"))
+            sc = ps.tile([P, I], F32, name="scores%d" % m, tag="bank_s%d" % m)
+            nc.tensor.matmul_mx(out=sc[:], lhsT=q_codes[:].bitcast(FP8X4), lhsT_scale=q_scales[:],
+                                rhs=k_codes[:].bitcast(FP8X4), rhs_scale=k_scales[:], start=True, stop=True)
+            scores.append(sc)
+
+        w_grouped = sb.tile([P, Q, PACK], BF16, name="w_grouped", align_bytes=64)
+        w_words = w_grouped[:].rearrange("p q j -> p (q j)").bitcast(F32).rearrange("p (q u) -> p q u", u=2)
+        for m in range(QT):
+            neg_max = sb.tile([P, 1], F32, name="neg_max%d" % m)
+            nc.vector.tensor_reduce(neg_max[:], scores[m][:], AXIS.X, ALU.max, negate=True)
+            probs = sb.tile([P, I], F32, name="probs%d" % m)
+            row_sum = sb.tile([P, 1], F32, name="row_sum%d" % m)
+            nc.scalar.activation(probs[:], scores[m][:], ACT.Exp, bias=neg_max[:], accum_out=row_sum[:])
+            inv_sum = sb.tile([P, 1], F32, name="inv_sum%d" % m)
+            nc.vector.reciprocal(inv_sum[:], row_sum[:])
+            w_rows = sb.tile([P, I], BF16, name="w_rows%d" % m)
+            nc.vector.scalar_tensor_tensor(w_rows[:], probs[:], inv_sum[:], size_all[:].rearrange("p s j -> p (s j)"), ALU.mult, ALU.mult)
+            w_ps = ps.tile([P, 2, P], F32, name="w_ps%d" % m, tag="bank_w%d" % m)
+            words = w_rows[:].bitcast(F32)
+            for u in range(2):
+                nc.tensor.transpose(w_ps[:, u, :], words[:, u : I // 2 : 2], ident[:])
+            nc.scalar.copy(w_words[:, m * P : (m + 1) * P, :], w_ps[:].rearrange("p u q -> p q u"))
+        w_codes = sb.tile([P, Q], U32, name="w_codes", align_bytes=64)
+        w_scales = sb.tile([P, Q], U8, name="w_scales", align_bytes=64)
+        nc.vector.quantize_mx(out=w_codes[:].bitcast(FP8X4), scales=w_scales[:], in_=w_grouped[:].rearrange("p q j -> p (q j)"))
+
+        out_v = out.rearrange("(p j) x -> p j x", j=PACK)
+        out_banks = ["bank_s0", "bank_s1", "bank_a", "bank_o"]
+        for j in range(PACK):
+            v_picked = sb.tile([P, I], BF16, name="v_picked%d" % j)
+            nc.vector.tensor_copy(v_picked[:], val_pool[j][:].indirect(lists[:]))
+            v_ps = ps.tile([P, 2, P], F32, name="v_ps%d" % j, tag="bank_v%d" % (j % 2))
+            words = v_picked[:].bitcast(F32)
+            for u in range(2):
+                nc.tensor.transpose(v_ps[:, u, :], words[:, u : I // 2 : 2], ident[:])
+            v_grouped = sb.tile([P, P * PACK], BF16, name="v_grouped%d" % j, align_bytes=64)
+            nc.scalar.copy(v_grouped[:].bitcast(F32).rearrange("p (e u) -> p e u", u=2), v_ps[:].rearrange("p u e -> p e u"))
+            v_codes = sb.tile([P, P], U32, name="v_codes%d" % j, align_bytes=64)
+            v_scales = sb.tile([P, P], U8, name="v_scales%d" % j, align_bytes=64)
+            nc.vector.quantize_mx(out=v_codes[:].bitcast(FP8X4), scales=v_scales[:], in_=v_grouped[:])
+            o_ps = ps.tile([P, Q], F32, name="o_ps%d" % j, tag=out_banks[j])
+            nc.tensor.matmul_mx(out=o_ps[:], lhsT=v_codes[:].bitcast(FP8X4), lhsT_scale=v_scales[:],
+                                rhs=w_codes[:].bitcast(FP8X4), rhs_scale=w_scales[:], start=True, stop=True)
+            masked = sb.tile([P, X, HEADS], F32, name="masked%d" % j)
+            nc.vector.tensor_tensor(masked[:].rearrange("p x h -> p (x h)"), o_ps[:], own_sb[:, j, :], ALU.mult)
+            result = sb.tile([P, X], F32, name="result%d" % j)
+            nc.vector.tensor_reduce(result[:], masked[:], AXIS.X, ALU.add)
+            nc.sync.dma_start(out_v[:, j, :], result[:])

@@ -28,103 +28,139 @@ def tile_attend_ownlists_heads_kernel(tc, query, keys, size, vals, own, offs, ou
         sb = ctx.enter_context(tc.tile_pool(name="sb", bufs=1))
         ps = ctx.enter_context(tc.psum_pool(name="ps", bufs=1))
 
-        lists = sb.tile([P, I // 16], U16, name="lists")
-        nc.sync.dma_start(lists[:], offs)
-        size_col = sb.tile([P, PACK], F32, name="size_col")
-        nc.sync.dma_start(size_col[:], size.rearrange("o (p j) -> (o p) j", j=PACK))
+        def alloc(shape, dtype, name, tag=None):
+            return sb.tile(shape, dtype, name=name, tag=tag or name, align_bytes=64)
+
+        lists = alloc([P, I // 16], U16, name="lists")
+        size_col = alloc([P, PACK], F32, name="size_col")
 
         keys_v = keys.rearrange("(p j) t -> p j t", j=PACK)
         vals_v = vals.rearrange("(p j) t -> p j t", j=PACK)
         key_pool = []
         for j in range(PACK):
-            kp = sb.tile([P, T], F32, name="key_pool%d" % j)
+            kp = alloc([P, T], F32, name="key_pool%d" % j)
             nc.sync.dma_start(kp[:], keys_v[:, j, :])
             key_pool.append(kp)
-        q_raw = sb.tile([P, PACK, Q], F32, name="q_raw")
+            if j == 0:
+                nc.sync.dma_start(lists[:], offs)
+                nc.sync.dma_start(size_col[:], size.rearrange("o (p j) -> (o p) j", j=PACK))
+        q_raw = alloc([P, PACK, Q], F32, name="q_raw")
         nc.sync.dma_start(q_raw[:], query.rearrange("(p j) q -> p j q", j=PACK))
         val_pool = []
         for j in range(PACK):
-            vp = sb.tile([P, T], F32, name="val_pool%d" % j)
+            vp = alloc([P, T], F32, name="val_pool%d" % j)
             nc.sync.dma_start(vp[:], vals_v[:, j, :])
             val_pool.append(vp)
-        own_sb = sb.tile([P, PACK, Q], F32, name="own_sb")
+        own_sb = alloc([P, PACK, Q], F32, name="own_sb")
         nc.sync.dma_start(own_sb[:], own.rearrange("(p j) q -> p j q", j=PACK))
 
-        ident = sb.tile([P, P], F32, name="ident")
+        ident = alloc([P, P], F32, name="ident")
         make_identity(nc, ident[:])
 
-        warm_in = sb.tile([P, 1], F32, name="warm_in")
-        warm_out = sb.tile([P, 1], F32, name="warm_out")
+        warm_in = alloc([P, 1], F32, name="warm_in")
+        warm_out = alloc([P, 1], F32, name="warm_out")
         nc.vector.memset(warm_in[:], 0.0)
         nc.scalar.activation(warm_out[:], warm_in[:], ACT.Exp)
 
         size_ps = ps.tile([P, PACK, P], F32, name="size_ps", tag="bank_a")
         for j in range(PACK):
             nc.tensor.transpose(size_ps[:, j, :], size_col[:, j : j + 1].to_broadcast([P, P]), ident[:])
-        size_all = sb.tile([P, P, PACK], F32, name="size_all")
+        size_all = alloc([P, P, PACK], F32, name="size_all")
         nc.scalar.copy(size_all[:], size_ps[:].rearrange("p j s -> p s j"))
 
-        k_grouped = sb.tile([P, I, PACK], BF16, name="k_grouped", align_bytes=64)
-        for j in range(PACK):
-            k_picked = sb.tile([P, I], BF16, name="k_picked%d" % j)
-            nc.vector.tensor_copy(k_picked[:], key_pool[j][:].indirect(lists[:]))
-            nc.vector.tensor_copy(k_grouped[:, :, j], k_picked[:])
-        k_codes = sb.tile([P, I], U32, name="k_codes", align_bytes=64)
-        k_scales = sb.tile([P, I], U8, name="k_scales", align_bytes=64)
-        nc.vector.quantize_mx(out=k_codes[:].bitcast(FP8X4), scales=k_scales[:], in_=k_grouped[:].rearrange("p i j -> p (i j)"))
+        k_grouped = alloc([P, I, PACK], BF16, name="k_grouped")
+        for u in range(2):
+            k_picked = alloc([P, 2, I], BF16, name="k_picked%d" % u)
+            for e in range(2):
+                nc.vector.tensor_copy(k_picked[:, e, :], key_pool[2 * u + e][:].indirect(lists[:]))
+            weave = nc.scalar.copy if u == 0 else nc.vector.tensor_copy
+            weave(k_grouped[:, :, 2 * u : 2 * u + 2], k_picked[:].rearrange("p e i -> p i e"))
+
+        def quantize(codes, scales, grouped):
+            nc.vector.quantize_mx(out=codes.bitcast(FP8X4), scales=scales, in_=grouped)
+
+        def product(bank, lhs_codes, lhs_scales, rhs_codes, rhs_scales):
+            nc.tensor.matmul_mx(out=bank, lhsT=lhs_codes.bitcast(FP8X4), lhsT_scale=lhs_scales,
+                                rhs=rhs_codes.bitcast(FP8X4), rhs_scale=rhs_scales, start=True, stop=True)
+
+        def turn(rows, grouped, name, bank):
+            turned = ps.tile([P, 2, P], F32, name=name, tag=bank)
+            words = rows.bitcast(F32)
+            for u in range(2):
+                nc.tensor.transpose(turned[:, u, :], words[:, u : I // 2 : 2], ident[:])
+            nc.scalar.copy(grouped.bitcast(F32).rearrange("p (c u) -> p c u", u=2), turned[:].rearrange("p u c -> p c u"))
+
+        def pick_values(j, tag):
+            picked = alloc([P, I], BF16, name="v_picked%d" % j, tag=tag)
+            nc.vector.tensor_copy(picked[:], val_pool[j][:].indirect(lists[:]))
+            return picked
+
+        q_codes = alloc([P, Q], U32, name="q_codes")
+        q_scales = alloc([P, Q], U8, name="q_scales")
+        q_grouped = []
+        for m in range(QT):
+            grouped = alloc([P, P, PACK], BF16, name="q_grouped%d" % m)
+            nc.scalar.copy(grouped[:], q_raw[:, :, m * P : (m + 1) * P].rearrange("p j q -> p q j"))
+            q_grouped.append(grouped[:].rearrange("p q j -> p (q j)"))
+        quantize(q_codes[:, 0:P], q_scales[:, 0:P], q_grouped[0])
+        k_codes = alloc([P, I], U32, name="k_codes", tag="q_grouped0")
+        k_scales = alloc([P, I], U8, name="k_scales")
+        quantize(k_codes[:], k_scales[:], k_grouped[:].rearrange("p i j -> p (i j)"))
+        quantize(q_codes[:, P:Q], q_scales[:, P:Q], q_grouped[1])
 
         scores = []
         for m in range(QT):
-            q_grouped = sb.tile([P, P, PACK], BF16, name="q_grouped%d" % m, align_bytes=64)
-            nc.scalar.copy(q_grouped[:], q_raw[:, :, m * P : (m + 1) * P].rearrange("p j q -> p q j"))
-            q_codes = sb.tile([P, P], U32, name="q_codes%d" % m, align_bytes=64)
-            q_scales = sb.tile([P, P], U8, name="q_scales%d" % m, align_bytes=64)
-            nc.vector.quantize_mx(out=q_codes[:].bitcast(FP8X4), scales=q_scales[:], in_=q_grouped[:].rearrange("p q j -> p (q j)"))
-            sc = ps.tile([P, I], F32, name="scores%d" % m, tag="bank_s%d" % m)
-            nc.tensor.matmul_mx(out=sc[:], lhsT=q_codes[:].bitcast(FP8X4), lhsT_scale=q_scales[:],
-                                rhs=k_codes[:].bitcast(FP8X4), rhs_scale=k_scales[:], start=True, stop=True)
-            scores.append(sc)
+            bank = ps.tile([P, I], F32, name="scores%d" % m, tag="bank_s%d" % m)
+            cols = slice(m * P, (m + 1) * P)
+            product(bank[:], q_codes[:, cols], q_scales[:, cols], k_codes[:], k_scales[:])
+            scores.append(bank)
 
-        w_grouped = sb.tile([P, Q, PACK], BF16, name="w_grouped", align_bytes=64)
-        w_words = w_grouped[:].rearrange("p q j -> p (q j)").bitcast(F32).rearrange("p (q u) -> p q u", u=2)
+        W = P * PACK
+        w_grouped = alloc([P, QT * W], BF16, name="w_grouped")
+        v_grouped = alloc([P, PACK * W], BF16, name="v_grouped")
+        picked0 = pick_values(0, "q_grouped1")
+        neg_max = alloc([P, QT], F32, name="neg_max", tag="val_pool0")
+        row_sum = alloc([P, QT], F32, name="row_sum")
+        probs = []
         for m in range(QT):
-            neg_max = sb.tile([P, 1], F32, name="neg_max%d" % m)
-            nc.vector.tensor_reduce(neg_max[:], scores[m][:], AXIS.X, ALU.max, negate=True)
-            probs = sb.tile([P, I], F32, name="probs%d" % m)
-            row_sum = sb.tile([P, 1], F32, name="row_sum%d" % m)
-            nc.scalar.activation(probs[:], scores[m][:], ACT.Exp, bias=neg_max[:], accum_out=row_sum[:])
-            inv_sum = sb.tile([P, 1], F32, name="inv_sum%d" % m)
-            nc.vector.reciprocal(inv_sum[:], row_sum[:])
-            w_rows = sb.tile([P, I], BF16, name="w_rows%d" % m)
-            nc.vector.scalar_tensor_tensor(w_rows[:], probs[:], inv_sum[:], size_all[:].rearrange("p s j -> p (s j)"), ALU.mult, ALU.mult)
-            w_ps = ps.tile([P, 2, P], F32, name="w_ps%d" % m, tag="bank_w%d" % m)
-            words = w_rows[:].bitcast(F32)
-            for u in range(2):
-                nc.tensor.transpose(w_ps[:, u, :], words[:, u : I // 2 : 2], ident[:])
-            nc.scalar.copy(w_words[:, m * P : (m + 1) * P, :], w_ps[:].rearrange("p u q -> p q u"))
-        w_codes = sb.tile([P, Q], U32, name="w_codes", align_bytes=64)
-        w_scales = sb.tile([P, Q], U8, name="w_scales", align_bytes=64)
-        nc.vector.quantize_mx(out=w_codes[:].bitcast(FP8X4), scales=w_scales[:], in_=w_grouped[:].rearrange("p q j -> p (q j)"))
+            nc.vector.tensor_reduce(neg_max[:, m : m + 1], scores[m][:], AXIS.X, ALU.max, negate=True)
+            p_rows = alloc([P, I], F32, name="probs%d" % m)
+            nc.scalar.activation(p_rows[:], scores[m][:], ACT.Exp, bias=neg_max[:, m : m + 1], accum_out=row_sum[:, m : m + 1])
+            probs.append(p_rows)
+        turn(picked0[:], v_grouped[:, 0:W], "v_turned0", "bank_v0")
+        picked1 = pick_values(1, None)
+        turn(picked1[:], v_grouped[:, W : 2 * W], "v_turned1", "bank_v1")
+        inv_sum = alloc([P, QT], F32, name="inv_sum", tag="val_pool1")
+        nc.vector.reciprocal(inv_sum[:], row_sum[:])
+        for m in range(QT):
+            w_rows = alloc([P, I], BF16, name="w_rows%d" % m)
+            nc.vector.scalar_tensor_tensor(w_rows[:], probs[m][:], inv_sum[:, m : m + 1],
+                                           size_all[:].rearrange("p s j -> p (s j)"), ALU.mult, ALU.mult)
+            turn(w_rows[:], w_grouped[:, m * W : (m + 1) * W], "w_turned%d" % m, "bank_w%d" % m)
+        picked2 = pick_values(2, "probs1")
+        turn(picked2[:], v_grouped[:, 2 * W : 3 * W], "v_turned2", "bank_v0")
+        picked3 = pick_values(3, "probs0")
+        turn(picked3[:], v_grouped[:, 3 * W : 4 * W], "v_turned3", "bank_v1")
+
+        codes = alloc([P, Q + PACK * P], U32, name="codes", tag="val_pool3")
+        w_scales = alloc([P, Q], U8, name="w_scales")
+        v_scales = alloc([P, PACK * P], U8, name="v_scales")
+        w_codes, v_codes = codes[:, 0:Q], codes[:, Q:]
+        quantize(w_codes, w_scales[:], w_grouped[:])
+        for first, last in ((0, 2), (2, 3), (3, 4)):
+            quantize(v_codes[:, first * P : last * P], v_scales[:, first * P : last * P], v_grouped[:, first * W : last * W])
 
         out_v = out.rearrange("(p j) x -> p j x", j=PACK)
-        out_banks = ["bank_s0", "bank_s1", "bank_a", "bank_o"]
-        for j in range(PACK):
-            v_picked = sb.tile([P, I], BF16, name="v_picked%d" % j)
-            nc.vector.tensor_copy(v_picked[:], val_pool[j][:].indirect(lists[:]))
-            v_ps = ps.tile([P, 2, P], F32, name="v_ps%d" % j, tag="bank_v%d" % (j % 2))
-            words = v_picked[:].bitcast(F32)
-            for u in range(2):
-                nc.tensor.transpose(v_ps[:, u, :], words[:, u : I // 2 : 2], ident[:])
-            v_grouped = sb.tile([P, P * PACK], BF16, name="v_grouped%d" % j, align_bytes=64)
-            nc.scalar.copy(v_grouped[:].bitcast(F32).rearrange("p (e u) -> p e u", u=2), v_ps[:].rearrange("p u e -> p e u"))
-            v_codes = sb.tile([P, P], U32, name="v_codes%d" % j, align_bytes=64)
-            v_scales = sb.tile([P, P], U8, name="v_scales%d" % j, align_bytes=64)
-            nc.vector.quantize_mx(out=v_codes[:].bitcast(FP8X4), scales=v_scales[:], in_=v_grouped[:])
-            o_ps = ps.tile([P, Q], F32, name="o_ps%d" % j, tag=out_banks[j])
-            nc.tensor.matmul_mx(out=o_ps[:], lhsT=v_codes[:].bitcast(FP8X4), lhsT_scale=v_scales[:],
-                                rhs=w_codes[:].bitcast(FP8X4), rhs_scale=w_scales[:], start=True, stop=True)
-            masked = sb.tile([P, X, HEADS], F32, name="masked%d" % j)
-            nc.vector.tensor_tensor(masked[:].rearrange("p x h -> p (x h)"), o_ps[:], own_sb[:, j, :], ALU.mult)
-            result = sb.tile([P, X], F32, name="result%d" % j)
-            nc.vector.tensor_reduce(result[:], masked[:], AXIS.X, ALU.add)
-            nc.sync.dma_start(out_v[:, j, :], result[:])
+        masked = []
+        for pair in range(2):
+            sums = ps.tile([P, 2, Q], F32, name="sums%d" % pair, tag="bank_s%d" % pair)
+            for e in range(2):
+                cols = slice((2 * pair + e) * P, (2 * pair + e + 1) * P)
+                product(sums[:, e, :], v_codes[:, cols], v_scales[:, cols], w_codes, w_scales[:])
+            tile = alloc([P, 2, Q], F32, name="masked%d" % pair)
+            nc.vector.tensor_tensor(tile[:], sums[:], own_sb[:, 2 * pair : 2 * pair + 2, :], ALU.mult)
+            masked.append(tile)
+        for pair in range(2):
+            result = alloc([P, 2, X], F32, name="result%d" % pair)
+            nc.vector.tensor_reduce(result[:].rearrange("p e x -> p (e x)"), masked[pair][:].rearrange("p e (x h) -> p (e x) h", h=HEADS), AXIS.X, ALU.add)
+            nc.sync.dma_start(out_v[:, 2 * pair : 2 * pair + 2, :], result[:])

@@ -26,6 +26,7 @@ def tile_attend_ownlists_heads_kernel(tc, query, keys, size, vals, own, offs, ou
     nc = tc.nc
     with ExitStack() as ctx:
         sb = ctx.enter_context(tc.tile_pool(name="sb", bufs=1))
+        shared = ctx.enter_context(tc.tile_pool(name="shared", bufs=1))
         ps = ctx.enter_context(tc.psum_pool(name="ps", bufs=1))
 
         def alloc(shape, dtype, name, tag=None):
@@ -48,7 +49,10 @@ def tile_attend_ownlists_heads_kernel(tc, query, keys, size, vals, own, offs, ou
         nc.sync.dma_start(q_raw[:], query.rearrange("(p j) q -> p j q", j=PACK))
         val_pool = []
         for j in range(PACK):
-            vp = alloc([P, T], F32, name="val_pool%d" % j)
+            if j == 1:
+                vp = shared.tile([P, T], F32, name="val_pool1", offset=0, align_bytes=64)
+            else:
+                vp = alloc([P, T], F32, name="val_pool%d" % j)
             nc.sync.dma_start(vp[:], vals_v[:, j, :])
             val_pool.append(vp)
         own_sb = alloc([P, PACK, Q], F32, name="own_sb")
@@ -68,13 +72,18 @@ def tile_attend_ownlists_heads_kernel(tc, query, keys, size, vals, own, offs, ou
         size_all = alloc([P, P, PACK], F32, name="size_all")
         nc.scalar.copy(size_all[:], size_ps[:].rearrange("p j s -> p s j"))
 
+        halves = (slice(0, I // 2), slice(I // 2, I))
         k_grouped = alloc([P, I, PACK], BF16, name="k_grouped")
         for u in range(2):
             k_picked = alloc([P, 2, I], BF16, name="k_picked%d" % u)
             for e in range(2):
                 nc.vector.tensor_copy(k_picked[:, e, :], key_pool[2 * u + e][:].indirect(lists[:]))
-            weave = nc.scalar.copy if u == 0 else nc.vector.tensor_copy
-            weave(k_grouped[:, :, 2 * u : 2 * u + 2], k_picked[:].rearrange("p e i -> p i e"))
+            pairs = k_picked[:].rearrange("p e i -> p i e")
+            if u == 0:
+                nc.scalar.copy(k_grouped[:, :, 0:2], pairs)
+            else:
+                for half in halves:
+                    nc.vector.tensor_copy(k_grouped[:, half, 2:4], pairs[:, half, :])
 
         def quantize(codes, scales, grouped):
             nc.vector.quantize_mx(out=codes.bitcast(FP8X4), scales=scales, in_=grouped)
@@ -95,18 +104,17 @@ def tile_attend_ownlists_heads_kernel(tc, query, keys, size, vals, own, offs, ou
             nc.vector.tensor_copy(picked[:], val_pool[j][:].indirect(lists[:]))
             return picked
 
+        k_codes = alloc([P, I], U32, name="k_codes")
+        k_scales = alloc([P, I], U8, name="k_scales")
+        for half in halves:
+            quantize(k_codes[:, half], k_scales[:, half], k_grouped[:, half, :].rearrange("p i j -> p (i j)"))
+        q_grouped = alloc([P, Q, PACK], BF16, name="q_grouped")
+        for m in range(QT):
+            cols = slice(m * P, (m + 1) * P)
+            nc.scalar.copy(q_grouped[:, cols, :], q_raw[:, :, cols].rearrange("p j q -> p q j"))
         q_codes = alloc([P, Q], U32, name="q_codes")
         q_scales = alloc([P, Q], U8, name="q_scales")
-        q_grouped = []
-        for m in range(QT):
-            grouped = alloc([P, P, PACK], BF16, name="q_grouped%d" % m)
-            nc.scalar.copy(grouped[:], q_raw[:, :, m * P : (m + 1) * P].rearrange("p j q -> p q j"))
-            q_grouped.append(grouped[:].rearrange("p q j -> p (q j)"))
-        quantize(q_codes[:, 0:P], q_scales[:, 0:P], q_grouped[0])
-        k_codes = alloc([P, I], U32, name="k_codes", tag="q_grouped0")
-        k_scales = alloc([P, I], U8, name="k_scales")
-        quantize(k_codes[:], k_scales[:], k_grouped[:].rearrange("p i j -> p (i j)"))
-        quantize(q_codes[:, P:Q], q_scales[:, P:Q], q_grouped[1])
+        quantize(q_codes[:], q_scales[:], q_grouped[:].rearrange("p q j -> p (q j)"))
 
         scores = []
         for m in range(QT):
@@ -117,8 +125,7 @@ def tile_attend_ownlists_heads_kernel(tc, query, keys, size, vals, own, offs, ou
 
         W = P * PACK
         w_grouped = alloc([P, QT * W], BF16, name="w_grouped")
-        v_grouped = alloc([P, PACK * W], BF16, name="v_grouped")
-        picked0 = pick_values(0, "q_grouped1")
+        picked0 = pick_values(0, None)
         neg_max = alloc([P, QT], F32, name="neg_max", tag="val_pool0")
         row_sum = alloc([P, QT], F32, name="row_sum")
         probs = []
@@ -127,40 +134,62 @@ def tile_attend_ownlists_heads_kernel(tc, query, keys, size, vals, own, offs, ou
             p_rows = alloc([P, I], F32, name="probs%d" % m)
             nc.scalar.activation(p_rows[:], scores[m][:], ACT.Exp, bias=neg_max[:, m : m + 1], accum_out=row_sum[:, m : m + 1])
             probs.append(p_rows)
-        turn(picked0[:], v_grouped[:, 0:W], "v_turned0", "bank_v0")
+        v_grouped01 = alloc([P, 2 * W], BF16, name="v_grouped01")
+        turn(picked0[:], v_grouped01[:, 0:W], "v_turned0", "bank_v0")
         picked1 = pick_values(1, None)
-        turn(picked1[:], v_grouped[:, W : 2 * W], "v_turned1", "bank_v1")
-        inv_sum = alloc([P, QT], F32, name="inv_sum", tag="val_pool1")
+        turn(picked1[:], v_grouped01[:, W:], "v_turned1", "bank_v1")
+        inv_sum = shared.tile([P, QT], F32, name="inv_sum", offset=0, align_bytes=64)
         nc.vector.reciprocal(inv_sum[:], row_sum[:])
+        v_scales01 = alloc([P, 2 * P], U8, name="v_scales01")
+        v_codes0 = shared.tile([P, P], U32, name="v_codes0", offset=64, align_bytes=64)
+        quantize(v_codes0[:], v_scales01[:, 0:P], v_grouped01[:, 0:W])
         for m in range(QT):
             w_rows = alloc([P, I], BF16, name="w_rows%d" % m)
             nc.vector.scalar_tensor_tensor(w_rows[:], probs[m][:], inv_sum[:, m : m + 1],
                                            size_all[:].rearrange("p s j -> p (s j)"), ALU.mult, ALU.mult)
             turn(w_rows[:], w_grouped[:, m * W : (m + 1) * W], "w_turned%d" % m, "bank_w%d" % m)
-        picked2 = pick_values(2, "probs1")
-        turn(picked2[:], v_grouped[:, 2 * W : 3 * W], "v_turned2", "bank_v0")
-        picked3 = pick_values(3, "probs0")
-        turn(picked3[:], v_grouped[:, 3 * W : 4 * W], "v_turned3", "bank_v1")
-
-        codes = alloc([P, Q + PACK * P], U32, name="codes", tag="val_pool3")
+        picked2 = pick_values(2, "probs0")
+        codes = alloc([P, P + Q], U32, name="codes", tag="val_pool2")
+        v_codes1, w_codes = codes[:, 0:P], codes[:, P:]
+        quantize(v_codes1, v_scales01[:, P:], v_grouped01[:, W:])
         w_scales = alloc([P, Q], U8, name="w_scales")
-        v_scales = alloc([P, PACK * P], U8, name="v_scales")
-        w_codes, v_codes = codes[:, 0:Q], codes[:, Q:]
         quantize(w_codes, w_scales[:], w_grouped[:])
-        for first, last in ((0, 2), (2, 3), (3, 4)):
-            quantize(v_codes[:, first * P : last * P], v_scales[:, first * P : last * P], v_grouped[:, first * W : last * W])
+        v_grouped2 = alloc([P, W], BF16, name="v_grouped2")
+        turn(picked2[:], v_grouped2[:], "v_turned2", "bank_v0")
+        sums01 = ps.tile([P, 2, Q], F32, name="sums01", tag="bank_s0")
+        for j, v_codes in enumerate((v_codes0[:], v_codes1)):
+            cols = slice(j * P, (j + 1) * P)
+            product(sums01[:, j, :], v_codes, v_scales01[:, cols], w_codes, w_scales[:])
+
+        picked3 = pick_values(3, "v_grouped01")
+        v_grouped3 = alloc([P, W], BF16, name="v_grouped3")
+        turn(picked3[:], v_grouped3[:], "v_turned3", "bank_v1")
+
+        def values_product(j, grouped, tag, bank):
+            v_codes = alloc([P, P], U32, name="v_codes%d" % j, tag=tag)
+            v_scales = alloc([P, P], U8, name="v_scales%d" % j)
+            quantize(v_codes[:], v_scales[:], grouped[:])
+            sums = ps.tile([P, 1, Q], F32, name="sums%d" % j, tag=bank)
+            product(sums[:, 0, :], v_codes[:], v_scales[:], w_codes, w_scales[:])
+            return sums
 
         out_v = out.rearrange("(p j) x -> p j x", j=PACK)
-        masked = []
-        for pair in range(2):
-            sums = ps.tile([P, 2, Q], F32, name="sums%d" % pair, tag="bank_s%d" % pair)
-            for e in range(2):
-                cols = slice((2 * pair + e) * P, (2 * pair + e + 1) * P)
-                product(sums[:, e, :], v_codes[:, cols], v_scales[:, cols], w_codes, w_scales[:])
-            tile = alloc([P, 2, Q], F32, name="masked%d" % pair)
-            nc.vector.tensor_tensor(tile[:], sums[:], own_sb[:, 2 * pair : 2 * pair + 2, :], ALU.mult)
-            masked.append(tile)
-        for pair in range(2):
-            result = alloc([P, 2, X], F32, name="result%d" % pair)
-            nc.vector.tensor_reduce(result[:].rearrange("p e x -> p (e x)"), masked[pair][:].rearrange("p e (x h) -> p (e x) h", h=HEADS), AXIS.X, ALU.add)
-            nc.sync.dma_start(out_v[:, 2 * pair : 2 * pair + 2, :], result[:])
+
+        def mask(first, count, sums, tag):
+            masked = alloc([P, count, Q], F32, name="masked%d" % first, tag=tag)
+            nc.vector.tensor_tensor(masked[:], sums[:], own_sb[:, first : first + count, :], ALU.mult)
+            return masked
+
+        def finish(first, count, masked, tag):
+            result = alloc([P, count, X], F32, name="result%d" % first, tag=tag)
+            nc.vector.tensor_reduce(result[:].rearrange("p e x -> p (e x)"), masked[:].rearrange("p e (x h) -> p (e x) h", h=HEADS), AXIS.X, ALU.add)
+            nc.sync.dma_start(out_v[:, first : first + count, :], result[:])
+
+        sums2 = values_product(2, v_grouped2, "val_pool3", "bank_s1")
+        masked01 = mask(0, 2, sums01, None)
+        masked2 = mask(2, 1, sums2, None)
+        sums3 = values_product(3, v_grouped3, None, "bank_a")
+        finish(0, 2, masked01, "v_grouped3")
+        finish(2, 1, masked2, None)
+        masked3 = mask(3, 1, sums3, None)
+        finish(3, 1, masked3, None)

from contextlib import ExitStack

import concourse.mybir as mybir
from concourse.masks import make_identity

D, T, I, Q, X, E = 512, 2048, 512, 256, 32, 512
FLOPS = 2 * Q * I * D + 2 * E * Q * I

F32 = mybir.dt.float32
BF16 = mybir.dt.bfloat16
U32 = mybir.dt.uint32
U16 = mybir.dt.uint16
U8 = mybir.dt.uint8
FP8X4 = mybir.dt.float8_e4m3fn_x4
ALU = mybir.AluOpType
ACT = mybir.ActivationFunctionType
AXIS = mybir.AxisListType

P = 128
PACK = 4
HEADS = Q // X
QT = Q // P


def tile_attend_ownlists_heads_kernel(tc, query, keys, size, vals, own, offs, out):
    nc = tc.nc
    with ExitStack() as ctx:
        sb = ctx.enter_context(tc.tile_pool(name="sb", bufs=1))
        shared = ctx.enter_context(tc.tile_pool(name="shared", bufs=1))
        ps = ctx.enter_context(tc.psum_pool(name="ps", bufs=1))

        def alloc(shape, dtype, name, tag=None):
            return sb.tile(shape, dtype, name=name, tag=tag or name, align_bytes=64)

        lists = alloc([P, I // 16], U16, name="lists")
        size_col = alloc([P, PACK], F32, name="size_col")

        keys_v = keys.rearrange("(p j) t -> p j t", j=PACK)
        vals_v = vals.rearrange("(p j) t -> p j t", j=PACK)
        key_pool = []
        for j in range(PACK):
            kp = alloc([P, T], F32, name="key_pool%d" % j)
            nc.sync.dma_start(kp[:], keys_v[:, j, :])
            key_pool.append(kp)
            if j == 0:
                nc.sync.dma_start(lists[:], offs)
                nc.sync.dma_start(size_col[:], size.rearrange("o (p j) -> (o p) j", j=PACK))
        q_raw = alloc([P, PACK, Q], F32, name="q_raw")
        nc.sync.dma_start(q_raw[:], query.rearrange("(p j) q -> p j q", j=PACK))
        val_pool = []
        for j in range(PACK):
            if j == 1:
                vp = shared.tile([P, T], F32, name="val_pool1", offset=0, align_bytes=64)
            else:
                vp = alloc([P, T], F32, name="val_pool%d" % j)
            nc.sync.dma_start(vp[:], vals_v[:, j, :])
            val_pool.append(vp)
        own_sb = alloc([P, PACK, Q], F32, name="own_sb")
        nc.sync.dma_start(own_sb[:], own.rearrange("(p j) q -> p j q", j=PACK))

        ident = alloc([P, P], F32, name="ident")
        make_identity(nc, ident[:])

        warm_in = alloc([P, 1], F32, name="warm_in")
        warm_out = alloc([P, 1], F32, name="warm_out")
        nc.vector.memset(warm_in[:], 0.0)
        nc.scalar.activation(warm_out[:], warm_in[:], ACT.Exp)

        size_ps = ps.tile([P, PACK, P], F32, name="size_ps", tag="bank_a")
        for j in range(PACK):
            nc.tensor.transpose(size_ps[:, j, :], size_col[:, j : j + 1].to_broadcast([P, P]), ident[:])
        size_all = alloc([P, P, PACK], F32, name="size_all")
        nc.scalar.copy(size_all[:], size_ps[:].rearrange("p j s -> p s j"))

        halves = (slice(0, I // 2), slice(I // 2, I))
        k_grouped = alloc([P, I, PACK], BF16, name="k_grouped")
        for u in range(2):
            k_picked = alloc([P, 2, I], BF16, name="k_picked%d" % u)
            for e in range(2):
                nc.vector.tensor_copy(k_picked[:, e, :], key_pool[2 * u + e][:].indirect(lists[:]))
            pairs = k_picked[:].rearrange("p e i -> p i e")
            if u == 0:
                nc.scalar.copy(k_grouped[:, :, 0:2], pairs)
            else:
                for half in halves:
                    nc.vector.tensor_copy(k_grouped[:, half, 2:4], pairs[:, half, :])

        def quantize(codes, scales, grouped):
            nc.vector.quantize_mx(out=codes.bitcast(FP8X4), scales=scales, in_=grouped)

        def product(bank, lhs_codes, lhs_scales, rhs_codes, rhs_scales):
            nc.tensor.matmul_mx(out=bank, lhsT=lhs_codes.bitcast(FP8X4), lhsT_scale=lhs_scales,
                                rhs=rhs_codes.bitcast(FP8X4), rhs_scale=rhs_scales, start=True, stop=True)

        def turn(rows, grouped, name, bank):
            turned = ps.tile([P, 2, P], F32, name=name, tag=bank)
            words = rows.bitcast(F32)
            for u in range(2):
                nc.tensor.transpose(turned[:, u, :], words[:, u : I // 2 : 2], ident[:])
            nc.scalar.copy(grouped.bitcast(F32).rearrange("p (c u) -> p c u", u=2), turned[:].rearrange("p u c -> p c u"))

        def pick_values(j, tag):
            picked = alloc([P, I], BF16, name="v_picked%d" % j, tag=tag)
            nc.vector.tensor_copy(picked[:], val_pool[j][:].indirect(lists[:]))
            return picked

        k_codes = alloc([P, I], U32, name="k_codes")
        k_scales = alloc([P, I], U8, name="k_scales")
        for half in halves:
            quantize(k_codes[:, half], k_scales[:, half], k_grouped[:, half, :].rearrange("p i j -> p (i j)"))
        q_grouped = alloc([P, Q, PACK], BF16, name="q_grouped")
        for m in range(QT):
            cols = slice(m * P, (m + 1) * P)
            nc.scalar.copy(q_grouped[:, cols, :], q_raw[:, :, cols].rearrange("p j q -> p q j"))
        q_codes = alloc([P, Q], U32, name="q_codes")
        q_scales = alloc([P, Q], U8, name="q_scales")
        quantize(q_codes[:], q_scales[:], q_grouped[:].rearrange("p q j -> p (q j)"))

        scores = []
        for m in range(QT):
            bank = ps.tile([P, I], F32, name="scores%d" % m, tag="bank_s%d" % m)
            cols = slice(m * P, (m + 1) * P)
            product(bank[:], q_codes[:, cols], q_scales[:, cols], k_codes[:], k_scales[:])
            scores.append(bank)

        W = P * PACK
        w_grouped = alloc([P, QT * W], BF16, name="w_grouped")
        picked0 = pick_values(0, None)
        neg_max = alloc([P, QT], F32, name="neg_max", tag="val_pool0")
        row_sum = alloc([P, QT], F32, name="row_sum")
        probs = []
        for m in range(QT):
            nc.vector.tensor_reduce(neg_max[:, m : m + 1], scores[m][:], AXIS.X, ALU.max, negate=True)
            p_rows = alloc([P, I], F32, name="probs%d" % m)
            nc.scalar.activation(p_rows[:], scores[m][:], ACT.Exp, bias=neg_max[:, m : m + 1], accum_out=row_sum[:, m : m + 1])
            probs.append(p_rows)
        v_grouped01 = alloc([P, 2 * W], BF16, name="v_grouped01")
        turn(picked0[:], v_grouped01[:, 0:W], "v_turned0", "bank_v0")
        picked1 = pick_values(1, None)
        turn(picked1[:], v_grouped01[:, W:], "v_turned1", "bank_v1")
        inv_sum = shared.tile([P, QT], F32, name="inv_sum", offset=0, align_bytes=64)
        nc.vector.reciprocal(inv_sum[:], row_sum[:])
        v_scales01 = alloc([P, 2 * P], U8, name="v_scales01")
        v_codes0 = shared.tile([P, P], U32, name="v_codes0", offset=64, align_bytes=64)
        quantize(v_codes0[:], v_scales01[:, 0:P], v_grouped01[:, 0:W])
        for m in range(QT):
            w_rows = alloc([P, I], BF16, name="w_rows%d" % m)
            nc.vector.scalar_tensor_tensor(w_rows[:], probs[m][:], inv_sum[:, m : m + 1],
                                           size_all[:].rearrange("p s j -> p (s j)"), ALU.mult, ALU.mult)
            turn(w_rows[:], w_grouped[:, m * W : (m + 1) * W], "w_turned%d" % m, "bank_w%d" % m)
        picked2 = pick_values(2, "probs0")
        codes = alloc([P, P + Q], U32, name="codes", tag="val_pool2")
        v_codes1, w_codes = codes[:, 0:P], codes[:, P:]
        quantize(v_codes1, v_scales01[:, P:], v_grouped01[:, W:])
        w_scales = alloc([P, Q], U8, name="w_scales")
        quantize(w_codes, w_scales[:], w_grouped[:])
        v_grouped2 = alloc([P, W], BF16, name="v_grouped2")
        turn(picked2[:], v_grouped2[:], "v_turned2", "bank_v0")
        sums01 = ps.tile([P, 2, Q], F32, name="sums01", tag="bank_s0")
        for j, v_codes in enumerate((v_codes0[:], v_codes1)):
            cols = slice(j * P, (j + 1) * P)
            product(sums01[:, j, :], v_codes, v_scales01[:, cols], w_codes, w_scales[:])

        picked3 = pick_values(3, "v_grouped01")
        v_grouped3 = alloc([P, W], BF16, name="v_grouped3")
        turn(picked3[:], v_grouped3[:], "v_turned3", "bank_v1")

        def values_product(j, grouped, tag, bank):
            v_codes = alloc([P, P], U32, name="v_codes%d" % j, tag=tag)
            v_scales = alloc([P, P], U8, name="v_scales%d" % j)
            quantize(v_codes[:], v_scales[:], grouped[:])
            sums = ps.tile([P, 1, Q], F32, name="sums%d" % j, tag=bank)
            product(sums[:, 0, :], v_codes[:], v_scales[:], w_codes, w_scales[:])
            return sums

        out_v = out.rearrange("(p j) x -> p j x", j=PACK)

        def mask(first, count, sums, tag):
            masked = alloc([P, count, Q], F32, name="masked%d" % first, tag=tag)
            nc.vector.tensor_tensor(masked[:], sums[:], own_sb[:, first : first + count, :], ALU.mult)
            return masked

        def finish(first, count, masked, tag):
            result = alloc([P, count, X], F32, name="result%d" % first, tag=tag)
            nc.vector.tensor_reduce(result[:].rearrange("p e x -> p (e x)"), masked[:].rearrange("p e (x h) -> p (e x) h", h=HEADS), AXIS.X, ALU.add)
            nc.sync.dma_start(out_v[:, first : first + count, :], result[:])

        sums2 = values_product(2, v_grouped2, "val_pool3", "bank_s1")
        masked01 = mask(0, 2, sums01, None)
        masked2 = mask(2, 1, sums2, None)
        sums3 = values_product(3, v_grouped3, None, "bank_a")
        finish(0, 2, masked01, "v_grouped3")
        finish(2, 1, masked2, None)
        masked3 = mask(3, 1, sums3, None)
        finish(3, 1, masked3, None)
